import numpy as np
import ml_dtypes


def mxq(x, axis, fmt="e4m3"):
    dtype, down = {"e4m3": (ml_dtypes.float8_e4m3fn, 7), "e5m2": (ml_dtypes.float8_e5m2, 14)}[fmt]
    v = np.moveaxis(np.asarray(x, np.float32).astype(ml_dtypes.bfloat16).astype(np.float64), axis, -1)
    blocks = v.reshape(v.shape[:-1] + (-1, 32))
    amax = np.abs(blocks).max(-1, keepdims=True)
    byte = np.maximum(np.where(amax > 0, np.frexp(amax)[1] - 1 + 127, 0) - down, 1)
    scale = np.exp2(byte - 127.0)
    codes = (blocks / scale).astype(np.float32).astype(dtype).astype(np.float64)
    return np.moveaxis((codes * scale).reshape(v.shape), -1, axis)


WIDE = False


def mx_kscale(k):
    if not WIDE:
        return np.ones(k)
    levels = np.array([10, -10, 5, -5, 0])
    if k % 512:
        return np.exp2(np.random.permutation(np.resize(levels, k // 32))).repeat(32)
    a = np.empty((k // 512, 16))
    for p in range(k // 512):
        a[p, :8] = np.random.permutation(np.resize(levels, 8))
        for g in range(8):
            far = levels[np.abs(levels - a[p, g]) >= 10]
            a[p, g + 8] = far[np.random.randint(len(far))]
    return np.exp2(a.ravel()).repeat(32)


def f64(x):
    return np.asarray(x).astype(np.float64)


def striped(idx):
    return np.tile(idx.reshape(-1, 16).T, (8, 1)).astype(np.uint16)


def unstriped(offs):
    return offs[:16].T.reshape(-1).astype(np.int64)


def pack_weight(w):
    k, n = w.shape
    w = f64(np.asarray(w, np.float32).astype(ml_dtypes.bfloat16)).reshape(k // 32, 32, n)
    amax = np.abs(w).max(1)
    byte = np.clip(np.where(amax > 0, np.frexp(amax)[1] - 1 + 127 - 7, 1), 1, 254)
    scaled = (w * np.exp2(127.0 - byte)[:, None, :]).reshape(k, n).astype(np.float32)
    words = np.ascontiguousarray(scaled.reshape(k // 512, 128, 4, n).transpose(0, 1, 3, 2)).astype(ml_dtypes.float8_e4m3fn).view(np.uint8)
    return words, np.ascontiguousarray(byte.astype(np.uint8).reshape(k // 512, 16, n))


def unpack_weight(words, scales):
    g, p, n, _ = words.shape
    vals = np.ascontiguousarray(words).view(ml_dtypes.float8_e4m3fn).astype(np.float64) * np.repeat(np.exp2(scales.astype(np.float64) - 127.0), 8, axis=1)[..., None]
    return vals.transpose(0, 1, 3, 2).reshape(g * 512, n)


def gelu(v):
    return 0.5 * v * (1.0 + np.tanh(np.sqrt(2.0 / np.pi) * (v + 0.044715 * v**3)))


K, T, E, C, N = 1024, 3072, 6, 128, 256


def by_expert(wq, xq):
    return np.concatenate([wq[e].T @ xq[:, e * C:(e + 1) * C] for e in range(E)], axis=1)


def setup_inputs():
    n = np.random.standard_normal
    s = mx_kscale(K)[:, None]
    packed = [pack_weight(m) for m in n((E, K, N)) / np.sqrt(K) / s[None]]
    return {
        "xT": (n((K, T)) * s).astype(np.float32),
        "w_words": np.stack([m[0] for m in packed]),
        "w_scales": np.stack([m[1] for m in packed]),
        "b": (0.3 * n((N, E))).astype(np.float32),
        "gate": np.tile(np.random.uniform(0.2, 1.0, E * C), (N, 1)).astype(np.float32),
        "offs": striped(np.random.permutation(T)[:E * C]),
    }


def reference(xT, w_words, w_scales, b, gate, offs):
    idx = unstriped(offs)
    xq = mxq(f64(xT)[:, idx], 0, "e4m3")
    w = np.stack([unpack_weight(w_words[e], w_scales[e]) for e in range(E)])
    y = by_expert(w, xq)
    y = gelu(y + np.repeat(f64(b), C, axis=1))
    out = np.zeros((N, T))
    out[:, idx] = f64(gate) * y
    return out

@@ -1,0 +1,133 @@
+from contextlib import ExitStack
+
+import concourse.mybir as mybir
+
+K, T, E, C, N = 1024, 3072, 6, 128, 256
+S = E * C
+P = 128
+PASSES = K // 512
+BLOCKS = N // P
+HALF = S // 2
+FLOPS = 2 * K * N * S
+
+F32 = mybir.dt.float32
+BF16 = mybir.dt.bfloat16
+I32 = mybir.dt.int32
+U32 = mybir.dt.uint32
+U16 = mybir.dt.uint16
+U8 = mybir.dt.uint8
+FP8X4 = mybir.dt.float8_e4m3fn_x4
+GELU = mybir.ActivationFunctionType.Gelu_apprx_tanh
+MULT = mybir.AluOpType.mult
+
+
+def tile_routed_moe_kernel(tc, xT, w_words, w_scales, b, gate, offs, out):
+    nc = tc.nc
+    with ExitStack() as ctx:
+        keep = ctx.enter_context(tc.tile_pool(name="keep", bufs=1))
+        psum = ctx.enter_context(tc.psum_pool(name="psum", bufs=8))
+
+        offsets = keep.tile([P, S // 16], U16, name="offsets")
+        bias = keep.tile([P, BLOCKS, E], F32, name="bias")
+        gates = keep.tile([P, BLOCKS, S], F32, name="gates")
+        words = keep.tile([P, E * PASSES, N], I32, name="words", align_bytes=64)
+        planes = keep.tile([P, E * PASSES, N], U8, name="planes", align_bytes=64)
+        warm = keep.tile([P, 1], F32, name="warm")
+        raw = [keep.tile([P, 2, T], F32, name=f"raw{i}", align_bytes=64) for i in range(2 * PASSES)]
+        pairs = [keep.tile([P, T, 2], BF16, name=f"pairs{i}", align_bytes=64) for i in range(2 * PASSES)]
+        slots = [keep.tile([P, S, 4], BF16, name=f"slots{a}", align_bytes=64) for a in range(PASSES)]
+        codes = [keep.tile([P, S], U32, name=f"codes{a}", align_bytes=64) for a in range(PASSES)]
+        scales = [keep.tile([P, S], U8, name=f"scales{a}", align_bytes=64) for a in range(PASSES)]
+        acts = [keep.tile([P, S], F32, name=f"acts{m}") for m in range(BLOCKS)]
+        window = [keep.tile([P, T], F32, name=f"window{m}") for m in range(BLOCKS)]
+
+        x_view = xT.rearrange("(g p u v) t -> g u p v t", p=P, u=2, v=2)
+        gate_view = gate.rearrange("(m p) s -> m p s", p=P)
+        out_view = out.rearrange("(m p) t -> m p t", p=P)
+        word_view = w_words.rearrange("e a p n r -> p (e a) (n r)").bitcast(I32)
+        plane_view = w_scales.rearrange("e a q n -> q (e a) n").bitcast(I32)
+
+        nc.scalar.dma_start(out=bias[:], in_=b.rearrange("(m p) e -> p m e", p=P))
+        nc.vector.memset(planes[:].bitcast(I32), 0)
+        nc.vector.memset(warm[:], 0.0)
+        nc.scalar.activation(warm[:], warm[:], GELU)
+        for m in range(BLOCKS):
+            nc.vector.memset(window[m][:], 0.0)
+
+        chunks = [[(0, T)], [(0, T)], [(0, T)], [(0, 1536), (1536, 2560), (2560, T)]]
+        for i in range(2 * PASSES):
+            for lo, hi in chunks[i]:
+                nc.sync.dma_start(out=raw[i][:, :, lo:hi], in_=x_view[i // 2, i % 2, :, :, lo:hi])
+            if i == 0:
+                nc.sync.dma_start(offsets[:], offs)
+        for q in range(4):
+            nc.sync.dma_start(out=planes[32 * q : 32 * q + 4].bitcast(I32), in_=plane_view[4 * q : 4 * q + 4])
+        half_ea = E * PASSES // 2
+        nc.sync.dma_start(out=words[:, 0:half_ea], in_=word_view[:, 0:half_ea])
+        nc.sync.dma_start(out=gates[:, 0], in_=gate_view[0])
+        nc.sync.dma_start(out=words[:, half_ea:], in_=word_view[:, half_ea:])
+        nc.sync.dma_start(out=gates[:, 1], in_=gate_view[1])
+
+        vector_share = {T: 2048, 1536: 1024, 1024: 640, 512: 384}
+
+        def cast(i):
+            for lo, hi in chunks[i]:
+                mid = lo + vector_share[hi - lo]
+                nc.vector.tensor_copy(pairs[i][:, lo:mid, :], raw[i][:, :, lo:mid].rearrange("p v t -> p t v"))
+                nc.scalar.copy(pairs[i][:, mid:hi, :], raw[i][:, :, mid:hi].rearrange("p v t -> p t v"))
+
+        def gather(i, lo, hi):
+            into = slots[i // 2][:].rearrange("p s r -> p (s r)").bitcast(U32).rearrange("p (s u) -> p s u", u=2)
+            table = pairs[i][:].rearrange("p t v -> p (t v)").bitcast(U32)
+            nc.vector.tensor_copy(into[:, lo:hi, i % 2], table.indirect(offsets[:, lo // 16 : hi // 16]))
+
+        def quantize(a, lo, hi):
+            nc.vector.quantize_mx(
+                out=codes[a][:, lo:hi].bitcast(FP8X4),
+                scales=scales[a][:, lo:hi],
+                in_=slots[a][:, lo:hi, :].rearrange("p s r -> p (s r)"),
+            )
+
+        def expert(m, e):
+            acc = psum.tile([P, C], F32, name="acc")
+            for a in range(PASSES):
+                ea = PASSES * e + a
+                cols = slice(m * P, (m + 1) * P)
+                sl = slice(e * C, (e + 1) * C)
+                nc.tensor.matmul_mx(
+                    out=acc[:],
+                    lhsT=words[:, ea, cols].bitcast(FP8X4),
+                    lhsT_scale=planes[:, ea, cols],
+                    rhs=codes[a][:, sl].bitcast(FP8X4),
+                    rhs_scale=scales[a][:, sl],
+                    start=(a == 0),
+                    stop=(a == PASSES - 1),
+                )
+            nc.scalar.activation(acts[m][:, e * C : (e + 1) * C], acc[:], GELU, bias=bias[:, m, e : e + 1])
+
+        def scatter(m, lo, hi):
+            nc.vector.tensor_tensor(
+                window[m][:].indirect(offsets[:, lo // 16 : hi // 16]), acts[m][:, lo:hi], gates[:, m, lo:hi], MULT
+            )
+
+        cast(0)
+        gather(0, 0, S)
+        cast(1)
+        gather(1, 0, S)
+        cast(2)
+        quantize(0, 0, 512)
+        quantize(0, 512, S)
+        gather(2, 0, S)
+        cast(3)
+        for h in range(2):
+            lo = h * HALF
+            gather(3, lo, lo + HALF)
+            quantize(1, lo, lo + 256)
+            quantize(1, lo + 256, lo + HALF)
+            for m in range(BLOCKS):
+                for e in range(3 * h, 3 * h + 3):
+                    expert(m, e)
+        for m in range(BLOCKS):
+            for h in range(2):
+                scatter(m, h * HALF, (h + 1) * HALF)
+            nc.sync.dma_start(out=out_view[m], in_=window[m][:])

@@ -54,7 +54,7 @@ def tile_routed_moe_kernel(tc, xT, w_words, w_scales, b, gate, offs, out):
         for m in range(BLOCKS):
             nc.vector.memset(window[m][:], 0.0)
 
-        chunks = [[(0, T)], [(0, T)], [(0, T)], [(0, 1536), (1536, 2560), (2560, T)]]
+        chunks = [[(0, T)], [(0, T)], [(0, T)], [(0, 1792), (1792, 2688), (2688, T)]]
         for i in range(2 * PASSES):
             for lo, hi in chunks[i]:
                 nc.sync.dma_start(out=raw[i][:, :, lo:hi], in_=x_view[i // 2, i % 2, :, :, lo:hi])
@@ -63,12 +63,13 @@ def tile_routed_moe_kernel(tc, xT, w_words, w_scales, b, gate, offs, out):
         for q in range(4):
             nc.sync.dma_start(out=planes[32 * q : 32 * q + 4].bitcast(I32), in_=plane_view[4 * q : 4 * q + 4])
         half_ea = E * PASSES // 2
-        nc.sync.dma_start(out=words[:, 0:half_ea], in_=word_view[:, 0:half_ea])
+        nc.sync.dma_start(out=words[:, 0:half_ea, 0:P], in_=word_view[:, 0:half_ea, 0:P])
         nc.sync.dma_start(out=gates[:, 0], in_=gate_view[0])
+        nc.sync.dma_start(out=words[:, 0:half_ea, P:N], in_=word_view[:, 0:half_ea, P:N])
         nc.sync.dma_start(out=words[:, half_ea:], in_=word_view[:, half_ea:])
         nc.sync.dma_start(out=gates[:, 1], in_=gate_view[1])
 
-        vector_share = {T: 2048, 1536: 1024, 1024: 640, 512: 384}
+        vector_share = {T: 2048, 1792: 1216, 896: 576, 384: 256}
 
         def cast(i):
             for lo, hi in chunks[i]:

@@ -54,7 +54,7 @@ def tile_routed_moe_kernel(tc, xT, w_words, w_scales, b, gate, offs, out):
         for m in range(BLOCKS):
             nc.vector.memset(window[m][:], 0.0)
 
-        chunks = [[(0, T)], [(0, T)], [(0, T)], [(0, 1792), (1792, 2688), (2688, T)]]
+        chunks = [[(0, T)], [(0, T)], [(0, T)], [(0, 1280), (1280, 2304), (2304, 2816), (2816, T)]]
         for i in range(2 * PASSES):
             for lo, hi in chunks[i]:
                 nc.sync.dma_start(out=raw[i][:, :, lo:hi], in_=x_view[i // 2, i % 2, :, :, lo:hi])
@@ -69,7 +69,7 @@ def tile_routed_moe_kernel(tc, xT, w_words, w_scales, b, gate, offs, out):
         nc.sync.dma_start(out=words[:, half_ea:], in_=word_view[:, half_ea:])
         nc.sync.dma_start(out=gates[:, 1], in_=gate_view[1])
 
-        vector_share = {T: 2048, 1792: 1216, 896: 576, 384: 256}
+        vector_share = {T: 1792, 1280: 640, 1024: 576, 512: 320, 256: 160}
 
         def cast(i):
             for lo, hi in chunks[i]:

from contextlib import ExitStack

import concourse.mybir as mybir

K, T, E, C, N = 1024, 3072, 6, 128, 256
S = E * C
P = 128
PASSES = K // 512
BLOCKS = N // P
HALF = S // 2
FLOPS = 2 * K * N * S

F32 = mybir.dt.float32
BF16 = mybir.dt.bfloat16
I32 = mybir.dt.int32
U32 = mybir.dt.uint32
U16 = mybir.dt.uint16
U8 = mybir.dt.uint8
FP8X4 = mybir.dt.float8_e4m3fn_x4
GELU = mybir.ActivationFunctionType.Gelu_apprx_tanh
MULT = mybir.AluOpType.mult


def tile_routed_moe_kernel(tc, xT, w_words, w_scales, b, gate, offs, out):
    nc = tc.nc
    with ExitStack() as ctx:
        keep = ctx.enter_context(tc.tile_pool(name="keep", bufs=1))
        psum = ctx.enter_context(tc.psum_pool(name="psum", bufs=8))

        offsets = keep.tile([P, S // 16], U16, name="offsets")
        bias = keep.tile([P, BLOCKS, E], F32, name="bias")
        gates = keep.tile([P, BLOCKS, S], F32, name="gates")
        words = keep.tile([P, E * PASSES, N], I32, name="words", align_bytes=64)
        planes = keep.tile([P, E * PASSES, N], U8, name="planes", align_bytes=64)
        warm = keep.tile([P, 1], F32, name="warm")
        raw = [keep.tile([P, 2, T], F32, name=f"raw{i}", align_bytes=64) for i in range(2 * PASSES)]
        pairs = [keep.tile([P, T, 2], BF16, name=f"pairs{i}", align_bytes=64) for i in range(2 * PASSES)]
        slots = [keep.tile([P, S, 4], BF16, name=f"slots{a}", align_bytes=64) for a in range(PASSES)]
        codes = [keep.tile([P, S], U32, name=f"codes{a}", align_bytes=64) for a in range(PASSES)]
        scales = [keep.tile([P, S], U8, name=f"scales{a}", align_bytes=64) for a in range(PASSES)]
        acts = [keep.tile([P, S], F32, name=f"acts{m}") for m in range(BLOCKS)]
        window = [keep.tile([P, T], F32, name=f"window{m}") for m in range(BLOCKS)]

        x_view = xT.rearrange("(g p u v) t -> g u p v t", p=P, u=2, v=2)
        gate_view = gate.rearrange("(m p) s -> m p s", p=P)
        out_view = out.rearrange("(m p) t -> m p t", p=P)
        word_view = w_words.rearrange("e a p n r -> p (e a) (n r)").bitcast(I32)
        plane_view = w_scales.rearrange("e a q n -> q (e a) n").bitcast(I32)

        nc.scalar.dma_start(out=bias[:], in_=b.rearrange("(m p) e -> p m e", p=P))
        nc.vector.memset(planes[:].bitcast(I32), 0)
        nc.vector.memset(warm[:], 0.0)
        nc.scalar.activation(warm[:], warm[:], GELU)
        for m in range(BLOCKS):
            nc.vector.memset(window[m][:], 0.0)

        chunks = [[(0, T)], [(0, T)], [(0, T)], [(0, 1280), (1280, 2304), (2304, 2816), (2816, T)]]
        for i in range(2 * PASSES):
            for lo, hi in chunks[i]:
                nc.sync.dma_start(out=raw[i][:, :, lo:hi], in_=x_view[i // 2, i % 2, :, :, lo:hi])
            if i == 0:
                nc.sync.dma_start(offsets[:], offs)
        for q in range(4):
            nc.sync.dma_start(out=planes[32 * q : 32 * q + 4].bitcast(I32), in_=plane_view[4 * q : 4 * q + 4])
        half_ea = E * PASSES // 2
        nc.sync.dma_start(out=words[:, 0:half_ea, 0:P], in_=word_view[:, 0:half_ea, 0:P])
        nc.sync.dma_start(out=gates[:, 0], in_=gate_view[0])
        nc.sync.dma_start(out=words[:, 0:half_ea, P:N], in_=word_view[:, 0:half_ea, P:N])
        nc.sync.dma_start(out=words[:, half_ea:], in_=word_view[:, half_ea:])
        nc.sync.dma_start(out=gates[:, 1], in_=gate_view[1])

        vector_share = {T: 1792, 1280: 640, 1024: 576, 512: 320, 256: 160}

        def cast(i):
            for lo, hi in chunks[i]:
                mid = lo + vector_share[hi - lo]
                nc.vector.tensor_copy(pairs[i][:, lo:mid, :], raw[i][:, :, lo:mid].rearrange("p v t -> p t v"))
                nc.scalar.copy(pairs[i][:, mid:hi, :], raw[i][:, :, mid:hi].rearrange("p v t -> p t v"))

        def gather(i, lo, hi):
            into = slots[i // 2][:].rearrange("p s r -> p (s r)").bitcast(U32).rearrange("p (s u) -> p s u", u=2)
            table = pairs[i][:].rearrange("p t v -> p (t v)").bitcast(U32)
            nc.vector.tensor_copy(into[:, lo:hi, i % 2], table.indirect(offsets[:, lo // 16 : hi // 16]))

        def quantize(a, lo, hi):
            nc.vector.quantize_mx(
                out=codes[a][:, lo:hi].bitcast(FP8X4),
                scales=scales[a][:, lo:hi],
                in_=slots[a][:, lo:hi, :].rearrange("p s r -> p (s r)"),
            )

        def expert(m, e):
            acc = psum.tile([P, C], F32, name="acc")
            for a in range(PASSES):
                ea = PASSES * e + a
                cols = slice(m * P, (m + 1) * P)
                sl = slice(e * C, (e + 1) * C)
                nc.tensor.matmul_mx(
                    out=acc[:],
                    lhsT=words[:, ea, cols].bitcast(FP8X4),
                    lhsT_scale=planes[:, ea, cols],
                    rhs=codes[a][:, sl].bitcast(FP8X4),
                    rhs_scale=scales[a][:, sl],
                    start=(a == 0),
                    stop=(a == PASSES - 1),
                )
            nc.scalar.activation(acts[m][:, e * C : (e + 1) * C], acc[:], GELU, bias=bias[:, m, e : e + 1])

        def scatter(m, lo, hi):
            nc.vector.tensor_tensor(
                window[m][:].indirect(offsets[:, lo // 16 : hi // 16]), acts[m][:, lo:hi], gates[:, m, lo:hi], MULT
            )

        cast(0)
        gather(0, 0, S)
        cast(1)
        gather(1, 0, S)
        cast(2)
        quantize(0, 0, 512)
        quantize(0, 512, S)
        gather(2, 0, S)
        cast(3)
        for h in range(2):
            lo = h * HALF
            gather(3, lo, lo + HALF)
            quantize(1, lo, lo + 256)
            quantize(1, lo + 256, lo + HALF)
            for m in range(BLOCKS):
                for e in range(3 * h, 3 * h + 3):
                    expert(m, e)
        for m in range(BLOCKS):
            for h in range(2):
                scatter(m, h * HALF, (h + 1) * HALF)
            nc.sync.dma_start(out=out_view[m], in_=window[m][:])
